import numpy as np
import ml_dtypes


def mxq(x, axis, fmt="e4m3"):
    dtype, down = {"e4m3": (ml_dtypes.float8_e4m3fn, 7), "e5m2": (ml_dtypes.float8_e5m2, 14)}[fmt]
    v = np.moveaxis(np.asarray(x, np.float32).astype(ml_dtypes.bfloat16).astype(np.float64), axis, -1)
    blocks = v.reshape(v.shape[:-1] + (-1, 32))
    amax = np.abs(blocks).max(-1, keepdims=True)
    byte = np.maximum(np.where(amax > 0, np.frexp(amax)[1] - 1 + 127, 0) - down, 1)
    scale = np.exp2(byte - 127.0)
    codes = (blocks / scale).astype(np.float32).astype(dtype).astype(np.float64)
    return np.moveaxis((codes * scale).reshape(v.shape), -1, axis)


WIDE = False


def mx_kscale(k):
    if not WIDE:
        return np.ones(k)
    levels = np.array([30, -30])
    if k % 512:
        return np.exp2(np.random.permutation(np.resize(levels, k // 32))).repeat(32)
    a = np.empty((k // 512, 16))
    for p in range(k // 512):
        a[p, :8] = np.random.permutation(np.resize(levels, 8))
        for g in range(8):
            far = levels[np.abs(levels - a[p, g]) >= 10]
            a[p, g + 8] = far[np.random.randint(len(far))]
    return np.exp2(a.ravel()).repeat(32)


def f64(x):
    return np.asarray(x).astype(np.float64)


E2M1 = np.array([0.0, 0.5, 1.0, 1.5, 2.0, 3.0, 4.0, 6.0, -0.0, -0.5, -1.0, -1.5, -2.0, -3.0, -4.0, -6.0])


def pack_weight(w, fmt):
    k, n = w.shape
    w = f64(np.asarray(w, np.float32).astype(ml_dtypes.bfloat16)).reshape(k // 32, 32, n)
    amax = np.abs(w).max(1)
    if fmt == "e4m3":
        byte = np.frexp(amax)[1] - 1 + 127 - 7
    else:
        mant, ex = np.frexp(amax / 6.0)
        byte = np.where(mant > 0.5, ex, ex - 1) + 127
    byte = np.clip(np.where(amax > 0, byte, 1), 1, 254)
    scaled = (w * np.exp2(127.0 - byte)[:, None, :]).reshape(k, n).astype(np.float32)
    by_word = np.ascontiguousarray(scaled.reshape(k // 512, 128, 4, n).transpose(0, 1, 3, 2))
    if fmt == "e4m3":
        words = by_word.astype(ml_dtypes.float8_e4m3fn).view(np.uint8)
    else:
        c = by_word.astype(ml_dtypes.float4_e2m1fn).view(np.uint8) & 0xF
        words = (c[..., 0::2] | (c[..., 1::2] << 4)).reshape(k // 512, 128, 2 * n)
    return np.ascontiguousarray(words), np.ascontiguousarray(byte.astype(np.uint8).reshape(k // 512, 16, n))


def unpack_weight(words, scales, fmt):
    g, _, n = scales.shape
    words = np.ascontiguousarray(words).reshape(g, 128, n, -1)
    if fmt == "e4m3":
        vals = words.view(ml_dtypes.float8_e4m3fn).astype(np.float64)
    else:
        nib = np.empty((g, 128, n, 4), np.uint8)
        nib[..., 0::2] = words & 0xF
        nib[..., 1::2] = words >> 4
        vals = E2M1[nib]
    vals = vals * np.repeat(np.exp2(scales.astype(np.float64) - 127.0), 8, axis=1)[..., None]
    return vals.transpose(0, 1, 3, 2).reshape(g * 512, n)


K, L, R, M, T = 1536, 1536, 512, 1536, 512


def setup_inputs():
    n = np.random.standard_normal
    s1 = mx_kscale(K)[:, None]
    s2 = mx_kscale(L)[:, None]
    u = mx_kscale(R)[:, None]
    p_w = pack_weight(n((R, M)) / np.sqrt(R) / u, "e2m1")
    return {
        "x": (n((K, T)) * s1).astype(np.float32),
        "wx": (n((K, R)) / np.sqrt(K) / s1 * u.T).astype(np.float32),
        "c": (n((L, T)) * s2).astype(np.float32),
        "wc": (n((L, R)) / np.sqrt(L) / s2).astype(np.float32),
        "w_words": p_w[0],
        "w_scales": p_w[1],
        "prev": (n((1536, 512))).astype(np.float32),
    }


def reference(x, wx, c, wc, w_words, w_scales, prev):
    x_ = mxq(f64(x), 0, "e4m3")
    wx_ = mxq(f64(wx), 0, "e4m3")
    c_ = mxq(f64(c), 0, "e5m2")
    wc_ = mxq(f64(wc), 0, "e4m3")
    w_ = unpack_weight(w_words, w_scales, "e2m1")
    h_ = mxq((wx_.T @ x_) * (wc_.T @ c_), 0, "e4m3")
    y = w_.T @ h_
    return f64(prev) + y

@@ -1,0 +1,195 @@
+from contextlib import ExitStack
+
+import concourse.mybir as mybir
+
+K, L, R, M, T = 1536, 1536, 512, 1536, 512
+FLOPS = 2 * (K * R * T + L * R * T + R * M * T)
+
+F32 = mybir.dt.float32
+BF16 = mybir.dt.bfloat16
+I32 = mybir.dt.int32
+U32 = mybir.dt.uint32
+U8 = mybir.dt.uint8
+E4M3 = mybir.dt.float8_e4m3fn_x4
+E5M2 = mybir.dt.float8_e5m2_x4
+E2M1 = mybir.dt.float4_e2m1fn_x4
+
+P = 128
+PACK = 4
+K_PASS = P * PACK
+PASSES = K // K_PASS
+CHUNK = 128
+CHUNKS = T // CHUNK
+N_TILES = M // P
+PREV_GROUP = 4
+
+
+def tile_mix_bilin_fm_res_kernel(tc, x, wx, c, wc, w_words, w_scales, prev, out):
+    nc = tc.nc
+    with ExitStack() as ctx:
+        sb = ctx.enter_context(tc.tile_pool(name="sb", bufs=1))
+        psum = ctx.enter_context(tc.psum_pool(name="psum", bufs=8))
+        ctx.enter_context(tc.manual_schedule())
+
+        def load_pass(src, g, name):
+            raw = sb.tile([P, PACK, T], F32, name=name)
+            nc.sync.dma_start(
+                out=raw[:], in_=src[g * K_PASS : (g + 1) * K_PASS, :].rearrange("(p j) w -> p j w", j=PACK)
+            )
+            return raw
+
+        def mx_tiles(name):
+            codes = sb.tile([P, T], U32, name=name + "_codes", align_bytes=64)
+            scales = sb.tile([P, T], U8, name=name + "_scales", align_bytes=64)
+            return codes, scales
+
+        def interleave(copy, dst, src):
+            copy(
+                out=dst.rearrange("p (c i j) -> p c j i", i=4, j=PACK),
+                in_=src.rearrange("p j (c i) -> p c j i", i=4),
+            )
+
+        def group_acts(raw):
+            grouped = sb.tile([P, PACK * T], BF16, name="grouped_acts", bufs=2, align_bytes=64)
+            interleave(nc.scalar.copy, grouped[:], raw[:])
+            return grouped
+
+        def group_weights(raw):
+            grouped = sb.tile([P, PACK * R], BF16, name="grouped_weights", bufs=2, align_bytes=64)
+            nc.vector.tensor_copy(
+                out=grouped[:].rearrange("p (s m j) -> p m j s", s=PACK, j=PACK),
+                in_=raw[:].rearrange("p j (m s) -> p m j s", s=PACK),
+            )
+            return grouped
+
+        def quantize(operand, fmt, grouped, cols=slice(0, T)):
+            codes, scales = operand
+            nc.vector.quantize_mx(out=codes[:, cols].bitcast(fmt), scales=scales[:, cols], in_=grouped[:])
+
+        def matmul(acc, lhs, lhs_cols, rhs, rhs_fmt, rhs_cols, start, stop):
+            nc.tensor.matmul_mx(
+                out=acc,
+                lhsT=lhs[0][:, lhs_cols].bitcast(E4M3),
+                lhsT_scale=lhs[1][:, lhs_cols],
+                rhs=rhs[0][:, rhs_cols].bitcast(rhs_fmt),
+                rhs_scale=rhs[1][:, rhs_cols],
+                start=start,
+                stop=stop,
+            )
+
+        def span(i, width):
+            return slice(i * width, (i + 1) * width)
+
+        w_plane = sb.tile([P, M], U8, align_bytes=64)
+        nc.vector.memset(w_plane[:].bitcast(I32), 0)
+        c_raw, wc_raw, x_raw, wx_raw = [], [], [], []
+        for g in range(PASSES):
+            c_raw.append(load_pass(c, g, "c_raw%d" % g))
+            if g == 0:
+                for q in range(4):
+                    nc.sync.dma_start(
+                        out=w_plane[32 * q : 32 * q + 4, :].bitcast(I32),
+                        in_=w_scales[0, 4 * q : 4 * q + 4, :].bitcast(I32),
+                    )
+            wc_raw.append(load_pass(wc, g, "wc_raw%d" % g))
+        for g in range(PASSES):
+            wx_raw.append(load_pass(wx, g, "wx_raw%d" % g))
+            x_raw.append(load_pass(x, g, "x_raw%d" % g))
+        w_codes = sb.tile([P, 2 * M], U8, align_bytes=64)
+        nc.sync.dma_start(out=w_codes[:].bitcast(I32), in_=w_words[0].bitcast(I32))
+        prev_sb = []
+        for g in range(N_TILES // PREV_GROUP):
+            rows = sb.tile([P, PREV_GROUP, T], F32, name="prev%d" % g)
+            nc.sync.dma_start(
+                out=rows[:], in_=prev[span(g, PREV_GROUP * P), :].rearrange("(i p) t -> p i t", p=P)
+            )
+            prev_sb.append(rows)
+
+        pc_banks = [psum.tile([P, T], F32, name="bank") for s in range(PACK)]
+        for g in range(PASSES):
+            c_q, wc_q = mx_tiles("c%d" % g), mx_tiles("wc%d" % g)
+            c_grouped = group_acts(c_raw[g])
+            wc_grouped = group_weights(wc_raw[g])
+            quantize(c_q, E5M2, c_grouped)
+            quantize(wc_q, E4M3, wc_grouped)
+            for s in range(PACK):
+                matmul(pc_banks[s][:], wc_q, span(s, P), c_q, E5M2, slice(0, T), g == 0, g == PASSES - 1)
+        pc_rows = sb.tile([P, PACK, T], F32)
+        for s in range(PACK):
+            nc.scalar.copy(out=pc_rows[:, s, :], in_=pc_banks[s][:])
+        pc_grouped = sb.tile([P, PACK * T], F32)
+
+        px_banks = [psum.tile([P, PACK, CHUNK], F32, name="bank") for b in range(CHUNKS)]
+
+        def px_pass(g, b, wx_q, x_q):
+            for s in range(PACK):
+                first = g == 0 and s == 0
+                last = g == PASSES - 1 and s == PACK - 1
+                matmul(px_banks[b][:, s, :], wx_q, span(s, P), x_q, E4M3, span(b, CHUNK), first, last)
+
+        for g in range(PASSES - 1):
+            wx_q, x_q = mx_tiles("wx%d" % g), mx_tiles("x%d" % g)
+            wx_grouped = group_weights(wx_raw[g])
+            x_grouped = group_acts(x_raw[g])
+            if g == 0:
+                interleave(nc.vector.tensor_copy, pc_grouped[:], pc_rows[:])
+            quantize(wx_q, E4M3, wx_grouped)
+            quantize(x_q, E4M3, x_grouped)
+            for b in range(CHUNKS):
+                px_pass(g, b, wx_q, x_q)
+
+        g = PASSES - 1
+        wx_q, x_q, h_q = mx_tiles("wx%d" % g), mx_tiles("x%d" % g), mx_tiles("h")
+        quantize(wx_q, E4M3, group_weights(wx_raw[g]))
+        x_chunks, h_chunks = [], []
+        for b in range(CHUNKS):
+            chunk = sb.tile([P, PACK * CHUNK], BF16, name="x_chunk%d" % b, align_bytes=64)
+            interleave(nc.vector.tensor_copy if b == 0 else nc.scalar.copy, chunk[:], x_raw[g][:, :, span(b, CHUNK)])
+            x_chunks.append(chunk)
+
+        def finish_px(b):
+            quantize(x_q, E4M3, x_chunks[b], span(b, CHUNK))
+            px_pass(g, b, wx_q, x_q)
+
+        def multiply(b):
+            chunk = sb.tile([P, PACK * CHUNK], BF16, name="h_chunk%d" % b, align_bytes=64)
+            nc.vector.tensor_tensor(
+                out=chunk[:].rearrange("p (t s) -> p t s", s=PACK),
+                in0=px_banks[b][:].rearrange("p s t -> p t s"),
+                in1=pc_grouped[:, span(b, PACK * CHUNK)].rearrange("p (t s) -> p t s", s=PACK),
+                op=mybir.AluOpType.mult,
+            )
+            h_chunks.append(chunk)
+
+        def quantize_h(b):
+            quantize(h_q, E4M3, h_chunks[b], span(b, CHUNK))
+
+        finish_px(0)
+        finish_px(1)
+        finish_px(2)
+        multiply(0)
+        finish_px(3)
+        multiply(1)
+        quantize_h(0)
+        multiply(2)
+        quantize_h(1)
+        multiply(3)
+        quantize_h(2)
+        quantize_h(3)
+
+        for i in range(N_TILES):
+            y = psum.tile([P, T], F32, name="bank")
+            nc.tensor.matmul_mx(
+                out=y[:],
+                lhsT=w_codes[:, span(i, 2 * P)].bitcast(E2M1),
+                lhsT_scale=w_plane[:, span(i, P)],
+                rhs=h_q[0][:].bitcast(E4M3),
+                rhs_scale=h_q[1][:],
+                start=True,
+                stop=True,
+            )
+            result = sb.tile([P, T], F32, name="result%d" % i)
+            nc.vector.tensor_tensor(
+                out=result[:], in0=y[:], in1=prev_sb[i // PREV_GROUP][:, i % PREV_GROUP, :], op=mybir.AluOpType.add
+            )
+            nc.sync.dma_start(out=out[span(i, P), :], in_=result[:])

@@ -21,7 +21,9 @@ PASSES = K // K_PASS
 CHUNK = 128
 CHUNKS = T // CHUNK
 N_TILES = M // P
-PREV_GROUP = 4
+PREV_GROUP = 6
+HALF = T // 2
+STORE_TILES = (1, 1, 2, 2, 2, 2, 1, 1)
 
 
 def tile_mix_bilin_fm_res_kernel(tc, x, wx, c, wc, w_words, w_scales, prev, out):
@@ -31,10 +33,10 @@ def tile_mix_bilin_fm_res_kernel(tc, x, wx, c, wc, w_words, w_scales, prev, out)
         psum = ctx.enter_context(tc.psum_pool(name="psum", bufs=8))
         ctx.enter_context(tc.manual_schedule())
 
-        def load_pass(src, g, name):
-            raw = sb.tile([P, PACK, T], F32, name=name)
+        def load_pass(src, g, name, cols=slice(0, T)):
+            raw = sb.tile([P, PACK, cols.stop - cols.start], F32, name=name)
             nc.sync.dma_start(
-                out=raw[:], in_=src[g * K_PASS : (g + 1) * K_PASS, :].rearrange("(p j) w -> p j w", j=PACK)
+                out=raw[:], in_=src[g * K_PASS : (g + 1) * K_PASS, cols].rearrange("(p j) w -> p j w", j=PACK)
             )
             return raw
 
@@ -81,20 +83,19 @@ def tile_mix_bilin_fm_res_kernel(tc, x, wx, c, wc, w_words, w_scales, prev, out)
             return slice(i * width, (i + 1) * width)
 
         w_plane = sb.tile([P, M], U8, align_bytes=64)
-        nc.vector.memset(w_plane[:].bitcast(I32), 0)
-        c_raw, wc_raw, x_raw, wx_raw = [], [], [], []
+        nc.gpsimd.memset(w_plane[:].bitcast(I32), 0)
+        for q in range(4):
+            nc.gpsimd.dma_start(
+                out=w_plane[32 * q : 32 * q + 4, :].bitcast(I32),
+                in_=w_scales[0, 4 * q : 4 * q + 4, :].bitcast(I32),
+            )
+        c_raw, wc_raw = [], []
         for g in range(PASSES):
             c_raw.append(load_pass(c, g, "c_raw%d" % g))
-            if g == 0:
-                for q in range(4):
-                    nc.sync.dma_start(
-                        out=w_plane[32 * q : 32 * q + 4, :].bitcast(I32),
-                        in_=w_scales[0, 4 * q : 4 * q + 4, :].bitcast(I32),
-                    )
             wc_raw.append(load_pass(wc, g, "wc_raw%d" % g))
-        for g in range(PASSES):
-            wx_raw.append(load_pass(wx, g, "wx_raw%d" % g))
-            x_raw.append(load_pass(x, g, "x_raw%d" % g))
+        wx_raw = [load_pass(wx, g, "wx_raw%d" % g) for g in range(PASSES)]
+        x_raw = [load_pass(x, g, "x_raw%d" % g) for g in range(PASSES - 1)]
+        x_last = [load_pass(x, PASSES - 1, "x_last%d" % u, span(u, HALF)) for u in range(2)]
         w_codes = sb.tile([P, 2 * M], U8, align_bytes=64)
         nc.sync.dma_start(out=w_codes[:].bitcast(I32), in_=w_words[0].bitcast(I32))
         prev_sb = []
@@ -118,6 +119,7 @@ def tile_mix_bilin_fm_res_kernel(tc, x, wx, c, wc, w_words, w_scales, prev, out)
         for s in range(PACK):
             nc.scalar.copy(out=pc_rows[:, s, :], in_=pc_banks[s][:])
         pc_grouped = sb.tile([P, PACK * T], F32)
+        interleave(nc.scalar.copy, pc_grouped[:], pc_rows[:])
 
         px_banks = [psum.tile([P, PACK, CHUNK], F32, name="bank") for b in range(CHUNKS)]
 
@@ -127,25 +129,32 @@ def tile_mix_bilin_fm_res_kernel(tc, x, wx, c, wc, w_words, w_scales, prev, out)
                 last = g == PASSES - 1 and s == PACK - 1
                 matmul(px_banks[b][:, s, :], wx_q, span(s, P), x_q, E4M3, span(b, CHUNK), first, last)
 
+        wx_qs = []
+        for g in range(PASSES):
+            wx_q = mx_tiles("wx%d" % g)
+            quantize(wx_q, E4M3, group_weights(wx_raw[g]))
+            wx_qs.append(wx_q)
+
         for g in range(PASSES - 1):
-            wx_q, x_q = mx_tiles("wx%d" % g), mx_tiles("x%d" % g)
-            wx_grouped = group_weights(wx_raw[g])
-            x_grouped = group_acts(x_raw[g])
-            if g == 0:
-                interleave(nc.vector.tensor_copy, pc_grouped[:], pc_rows[:])
-            quantize(wx_q, E4M3, wx_grouped)
-            quantize(x_q, E4M3, x_grouped)
-            for b in range(CHUNKS):
-                px_pass(g, b, wx_q, x_q)
+            x_q = mx_tiles("x%d" % g)
+            halves = []
+            for u, copy in enumerate((nc.scalar.copy, nc.vector.tensor_copy)):
+                half = sb.tile([P, PACK * HALF], BF16, name="x_half%d" % u, bufs=2, align_bytes=64)
+                interleave(copy, half[:], x_raw[g][:, :, span(u, HALF)])
+                halves.append(half)
+            for u in (1, 0):
+                quantize(x_q, E4M3, halves[u], span(u, HALF))
+                for b in (2 * u, 2 * u + 1):
+                    px_pass(g, b, wx_qs[g], x_q)
 
         g = PASSES - 1
-        wx_q, x_q, h_q = mx_tiles("wx%d" % g), mx_tiles("x%d" % g), mx_tiles("h")
-        quantize(wx_q, E4M3, group_weights(wx_raw[g]))
-        x_chunks, h_chunks = [], []
-        for b in range(CHUNKS):
+        wx_q, x_q, h_q = wx_qs[g], mx_tiles("x%d" % g), mx_tiles("h")
+        x_chunks, h_chunks = {}, []
+
+        def group_chunk(copy, b):
             chunk = sb.tile([P, PACK * CHUNK], BF16, name="x_chunk%d" % b, align_bytes=64)
-            interleave(nc.vector.tensor_copy if b == 0 else nc.scalar.copy, chunk[:], x_raw[g][:, :, span(b, CHUNK)])
-            x_chunks.append(chunk)
+            interleave(copy, chunk[:], x_last[b // 2][:, :, span(b % 2, CHUNK)])
+            x_chunks[b] = chunk
 
         def finish_px(b):
             quantize(x_q, E4M3, x_chunks[b], span(b, CHUNK))
@@ -164,10 +173,14 @@ def tile_mix_bilin_fm_res_kernel(tc, x, wx, c, wc, w_words, w_scales, prev, out)
         def quantize_h(b):
             quantize(h_q, E4M3, h_chunks[b], span(b, CHUNK))
 
+        group_chunk(nc.vector.tensor_copy, 0)
+        group_chunk(nc.scalar.copy, 1)
+        group_chunk(nc.scalar.copy, 3)
         finish_px(0)
         finish_px(1)
-        finish_px(2)
+        group_chunk(nc.vector.tensor_copy, 2)
         multiply(0)
+        finish_px(2)
         finish_px(3)
         multiply(1)
         quantize_h(0)
@@ -177,19 +190,26 @@ def tile_mix_bilin_fm_res_kernel(tc, x, wx, c, wc, w_words, w_scales, prev, out)
         quantize_h(2)
         quantize_h(3)
 
-        for i in range(N_TILES):
-            y = psum.tile([P, T], F32, name="bank")
-            nc.tensor.matmul_mx(
-                out=y[:],
-                lhsT=w_codes[:, span(i, 2 * P)].bitcast(E2M1),
-                lhsT_scale=w_plane[:, span(i, P)],
-                rhs=h_q[0][:].bitcast(E4M3),
-                rhs_scale=h_q[1][:],
-                start=True,
-                stop=True,
-            )
-            result = sb.tile([P, T], F32, name="result%d" % i)
-            nc.vector.tensor_tensor(
-                out=result[:], in0=y[:], in1=prev_sb[i // PREV_GROUP][:, i % PREV_GROUP, :], op=mybir.AluOpType.add
-            )
-            nc.sync.dma_start(out=out[span(i, P), :], in_=result[:])
+        first = 0
+        for count in STORE_TILES:
+            result = sb.tile([P, count, T], F32, name="result%d" % first)
+            for i in range(first, first + count):
+                y = psum.tile([P, T], F32, name="bank")
+                nc.tensor.matmul_mx(
+                    out=y[:],
+                    lhsT=w_codes[:, span(i, 2 * P)].bitcast(E2M1),
+                    lhsT_scale=w_plane[:, span(i, P)],
+                    rhs=h_q[0][:].bitcast(E4M3),
+                    rhs_scale=h_q[1][:],
+                    start=True,
+                    stop=True,
+                )
+                nc.vector.tensor_tensor(
+                    out=result[:, i - first, :],
+                    in0=y[:],
+                    in1=prev_sb[i // PREV_GROUP][:, i % PREV_GROUP, :],
+                    op=mybir.AluOpType.add,
+                )
+            rows = out[first * P : (first + count) * P, :]
+            nc.sync.dma_start(out=rows.rearrange("(i p) t -> p i t", p=P), in_=result[:])
+            first = first + count

@@ -21,9 +21,9 @@ PASSES = K // K_PASS
 CHUNK = 128
 CHUNKS = T // CHUNK
 N_TILES = M // P
-PREV_GROUP = 6
+PREV_GROUP = 4
 HALF = T // 2
-STORE_TILES = (1, 1, 2, 2, 2, 2, 1, 1)
+STORE_TILES = (1,) * N_TILES
 
 
 def tile_mix_bilin_fm_res_kernel(tc, x, wx, c, wc, w_words, w_scales, prev, out):
@@ -57,12 +57,19 @@ def tile_mix_bilin_fm_res_kernel(tc, x, wx, c, wc, w_words, w_scales, prev, out)
             return grouped
 
         def group_weights(raw):
-            grouped = sb.tile([P, PACK * R], BF16, name="grouped_weights", bufs=2, align_bytes=64)
-            nc.vector.tensor_copy(
-                out=grouped[:].rearrange("p (s m j) -> p m j s", s=PACK, j=PACK),
-                in_=raw[:].rearrange("p j (m s) -> p m j s", s=PACK),
-            )
-            return grouped
+            halves = []
+            for u in range(2):
+                half = sb.tile([P, 2 * PACK * P], BF16, name="weight_half%d" % u, bufs=2, align_bytes=64)
+                nc.vector.tensor_copy(
+                    out=half[:].rearrange("p (s m j) -> p m j s", s=2, j=PACK),
+                    in_=raw[:].rearrange("p j (m s) -> p m j s", s=PACK)[:, :, :, 2 * u : 2 * u + 2],
+                )
+                halves.append(half)
+            return halves
+
+        def quantize_weights(operand, halves):
+            for u in range(2):
+                quantize(operand, E4M3, halves[u], span(u, R // 2))
 
         def quantize(operand, fmt, grouped, cols=slice(0, T)):
             codes, scales = operand
@@ -83,19 +90,19 @@ def tile_mix_bilin_fm_res_kernel(tc, x, wx, c, wc, w_words, w_scales, prev, out)
             return slice(i * width, (i + 1) * width)
 
         w_plane = sb.tile([P, M], U8, align_bytes=64)
-        nc.gpsimd.memset(w_plane[:].bitcast(I32), 0)
-        for q in range(4):
-            nc.gpsimd.dma_start(
-                out=w_plane[32 * q : 32 * q + 4, :].bitcast(I32),
-                in_=w_scales[0, 4 * q : 4 * q + 4, :].bitcast(I32),
-            )
+        nc.vector.memset(w_plane[:].bitcast(I32), 0)
         c_raw, wc_raw = [], []
         for g in range(PASSES):
             c_raw.append(load_pass(c, g, "c_raw%d" % g))
+            if g == 0:
+                for q in range(4):
+                    nc.sync.dma_start(
+                        out=w_plane[32 * q : 32 * q + 4, :].bitcast(I32),
+                        in_=w_scales[0, 4 * q : 4 * q + 4, :].bitcast(I32),
+                    )
             wc_raw.append(load_pass(wc, g, "wc_raw%d" % g))
         wx_raw = [load_pass(wx, g, "wx_raw%d" % g) for g in range(PASSES)]
-        x_raw = [load_pass(x, g, "x_raw%d" % g) for g in range(PASSES - 1)]
-        x_last = [load_pass(x, PASSES - 1, "x_last%d" % u, span(u, HALF)) for u in range(2)]
+        x_raw = [load_pass(x, g, "x_raw%d" % g) for g in range(PASSES)]
         w_codes = sb.tile([P, 2 * M], U8, align_bytes=64)
         nc.sync.dma_start(out=w_codes[:].bitcast(I32), in_=w_words[0].bitcast(I32))
         prev_sb = []
@@ -112,7 +119,7 @@ def tile_mix_bilin_fm_res_kernel(tc, x, wx, c, wc, w_words, w_scales, prev, out)
             c_grouped = group_acts(c_raw[g])
             wc_grouped = group_weights(wc_raw[g])
             quantize(c_q, E5M2, c_grouped)
-            quantize(wc_q, E4M3, wc_grouped)
+            quantize_weights(wc_q, wc_grouped)
             for s in range(PACK):
                 matmul(pc_banks[s][:], wc_q, span(s, P), c_q, E5M2, slice(0, T), g == 0, g == PASSES - 1)
         pc_rows = sb.tile([P, PACK, T], F32)
@@ -132,7 +139,7 @@ def tile_mix_bilin_fm_res_kernel(tc, x, wx, c, wc, w_words, w_scales, prev, out)
         wx_qs = []
         for g in range(PASSES):
             wx_q = mx_tiles("wx%d" % g)
-            quantize(wx_q, E4M3, group_weights(wx_raw[g]))
+            quantize_weights(wx_q, group_weights(wx_raw[g]))
             wx_qs.append(wx_q)
 
         for g in range(PASSES - 1):
@@ -153,7 +160,7 @@ def tile_mix_bilin_fm_res_kernel(tc, x, wx, c, wc, w_words, w_scales, prev, out)
 
         def group_chunk(copy, b):
             chunk = sb.tile([P, PACK * CHUNK], BF16, name="x_chunk%d" % b, align_bytes=64)
-            interleave(copy, chunk[:], x_last[b // 2][:, :, span(b % 2, CHUNK)])
+            interleave(copy, chunk[:], x_raw[g][:, :, span(b, CHUNK)])
             x_chunks[b] = chunk
 
         def finish_px(b):
@@ -174,13 +181,12 @@ def tile_mix_bilin_fm_res_kernel(tc, x, wx, c, wc, w_words, w_scales, prev, out)
             quantize(h_q, E4M3, h_chunks[b], span(b, CHUNK))
 
         group_chunk(nc.vector.tensor_copy, 0)
-        group_chunk(nc.scalar.copy, 1)
-        group_chunk(nc.scalar.copy, 3)
+        for b in range(1, CHUNKS):
+            group_chunk(nc.scalar.copy, b)
         finish_px(0)
         finish_px(1)
-        group_chunk(nc.vector.tensor_copy, 2)
-        multiply(0)
         finish_px(2)
+        multiply(0)
         finish_px(3)
         multiply(1)
         quantize_h(0)

@@ -23,7 +23,8 @@ CHUNKS = T // CHUNK
 N_TILES = M // P
 PREV_GROUP = 4
 HALF = T // 2
-STORE_TILES = (1,) * N_TILES
+STORE_TILES = (1, 1, 2, 2, 2, 2, 1, 1)
+SPLIT_TILES = 2
 
 
 def tile_mix_bilin_fm_res_kernel(tc, x, wx, c, wc, w_words, w_scales, prev, out):
@@ -89,29 +90,40 @@ def tile_mix_bilin_fm_res_kernel(tc, x, wx, c, wc, w_words, w_scales, prev, out)
         def span(i, width):
             return slice(i * width, (i + 1) * width)
 
-        w_plane = sb.tile([P, M], U8, align_bytes=64)
-        nc.vector.memset(w_plane[:].bitcast(I32), 0)
+        plane_raw = sb.tile([P, M], U8)
+        nc.vector.memset(plane_raw[:].bitcast(I32), 0)
+        words_raw = sb.tile([P, 2 * M], U8)
+        nc.sync.dma_start(out=words_raw[:].bitcast(I32), in_=w_words[0].bitcast(I32))
         c_raw, wc_raw = [], []
         for g in range(PASSES):
             c_raw.append(load_pass(c, g, "c_raw%d" % g))
             if g == 0:
                 for q in range(4):
                     nc.sync.dma_start(
-                        out=w_plane[32 * q : 32 * q + 4, :].bitcast(I32),
+                        out=plane_raw[32 * q : 32 * q + 4, :].bitcast(I32),
                         in_=w_scales[0, 4 * q : 4 * q + 4, :].bitcast(I32),
                     )
             wc_raw.append(load_pass(wc, g, "wc_raw%d" % g))
         wx_raw = [load_pass(wx, g, "wx_raw%d" % g) for g in range(PASSES)]
         x_raw = [load_pass(x, g, "x_raw%d" % g) for g in range(PASSES)]
-        w_codes = sb.tile([P, 2 * M], U8, align_bytes=64)
-        nc.sync.dma_start(out=w_codes[:].bitcast(I32), in_=w_words[0].bitcast(I32))
         prev_sb = []
         for g in range(N_TILES // PREV_GROUP):
             rows = sb.tile([P, PREV_GROUP, T], F32, name="prev%d" % g)
             nc.sync.dma_start(
-                out=rows[:], in_=prev[span(g, PREV_GROUP * P), :].rearrange("(i p) t -> p i t", p=P)
+                out=rows[:], in_=prev[span(g, PREV_GROUP * P), :].rearrange("(p i) t -> p i t", p=P)
             )
             prev_sb.append(rows)
+
+        w_codes = sb.tile([P, 2 * M], U8, align_bytes=64)
+        w_plane = sb.tile([P, M], U8, align_bytes=64)
+        nc.vector.tensor_copy(
+            out=w_codes[:].rearrange("p (g i m b) -> p g m i b", i=PREV_GROUP, m=P, b=2),
+            in_=words_raw[:].rearrange("p (g m i b) -> p g m i b", i=PREV_GROUP, m=P, b=2),
+        )
+        nc.vector.tensor_copy(
+            out=w_plane[:].rearrange("p (g i m) -> p g m i", i=PREV_GROUP, m=P),
+            in_=plane_raw[:].rearrange("p (g m i) -> p g m i", i=PREV_GROUP, m=P),
+        )
 
         pc_banks = [psum.tile([P, T], F32, name="bank") for s in range(PACK)]
         for g in range(PASSES):
@@ -180,42 +192,80 @@ def tile_mix_bilin_fm_res_kernel(tc, x, wx, c, wc, w_words, w_scales, prev, out)
         def quantize_h(b):
             quantize(h_q, E4M3, h_chunks[b], span(b, CHUNK))
 
+        def y_matmul(bank, i, cols):
+            nc.tensor.matmul_mx(
+                out=bank[:, cols],
+                lhsT=w_codes[:, span(i, 2 * P)].bitcast(E2M1),
+                lhsT_scale=w_plane[:, span(i, P)],
+                rhs=h_q[0][:, cols].bitcast(E4M3),
+                rhs_scale=h_q[1][:, cols],
+                start=True,
+                stop=True,
+            )
+
+        results, stores = [], {}
+        for count in STORE_TILES:
+            first = len(results)
+            result = sb.tile([P, count, T], F32, name="result%d" % first)
+            results.extend(result[:, j, :] for j in range(count))
+            group, slot = divmod(first, PREV_GROUP)
+            rows = out[span(group, PREV_GROUP * P), :].rearrange("(p i) t -> p i t", p=P)
+            stores[first + count - 1] = (rows[:, slot : slot + count, :], result)
+
+        def add_prev(bank, i, cols, bank_cols):
+            nc.vector.tensor_tensor(
+                out=results[i][:, cols],
+                in0=bank[:, bank_cols],
+                in1=prev_sb[i // PREV_GROUP][:, i % PREV_GROUP, cols],
+                op=mybir.AluOpType.add,
+            )
+            if cols.stop == T and i in stores:
+                rows, result = stores[i]
+                nc.sync.dma_start(out=rows, in_=result[:])
+
+        def y_half_matmul(bank, i, u):
+            nc.tensor.matmul_mx(
+                out=bank[:, span(i, HALF)],
+                lhsT=w_codes[:, span(i, 2 * P)].bitcast(E2M1),
+                lhsT_scale=w_plane[:, span(i, P)],
+                rhs=h_q[0][:, span(u, HALF)].bitcast(E4M3),
+                rhs_scale=h_q[1][:, span(u, HALF)],
+                start=True,
+                stop=True,
+            )
+
         group_chunk(nc.vector.tensor_copy, 0)
-        for b in range(1, CHUNKS):
-            group_chunk(nc.scalar.copy, b)
-        finish_px(0)
-        finish_px(1)
-        finish_px(2)
+        group_chunk(nc.vector.tensor_copy, 1)
+        group_chunk(nc.scalar.copy, 2)
+        group_chunk(nc.scalar.copy, 3)
+        for b in range(CHUNKS):
+            finish_px(b)
         multiply(0)
-        finish_px(3)
         multiply(1)
         quantize_h(0)
         multiply(2)
         quantize_h(1)
+        early = psum.tile([P, T], F32, name="bank")
+        for i in range(SPLIT_TILES):
+            y_half_matmul(early, i, 0)
         multiply(3)
         quantize_h(2)
         quantize_h(3)
-
-        first = 0
-        for count in STORE_TILES:
-            result = sb.tile([P, count, T], F32, name="result%d" % first)
-            for i in range(first, first + count):
-                y = psum.tile([P, T], F32, name="bank")
-                nc.tensor.matmul_mx(
-                    out=y[:],
-                    lhsT=w_codes[:, span(i, 2 * P)].bitcast(E2M1),
-                    lhsT_scale=w_plane[:, span(i, P)],
-                    rhs=h_q[0][:].bitcast(E4M3),
-                    rhs_scale=h_q[1][:],
-                    start=True,
-                    stop=True,
-                )
-                nc.vector.tensor_tensor(
-                    out=result[:, i - first, :],
-                    in0=y[:],
-                    in1=prev_sb[i // PREV_GROUP][:, i % PREV_GROUP, :],
-                    op=mybir.AluOpType.add,
-                )
-            rows = out[first * P : (first + count) * P, :]
-            nc.sync.dma_start(out=rows.rearrange("(i p) t -> p i t", p=P), in_=result[:])
-            first = first + count
+        for i in range(SPLIT_TILES):
+            add_prev(early, i, span(0, HALF), span(i, HALF))
+        for i in range(SPLIT_TILES):
+            late = psum.tile([P, HALF], F32, name="bank")
+            nc.tensor.matmul_mx(
+                out=late[:],
+                lhsT=w_codes[:, span(i, 2 * P)].bitcast(E2M1),
+                lhsT_scale=w_plane[:, span(i, P)],
+                rhs=h_q[0][:, span(1, HALF)].bitcast(E4M3),
+                rhs_scale=h_q[1][:, span(1, HALF)],
+                start=True,
+                stop=True,
+            )
+            add_prev(late, i, span(1, HALF), span(0, HALF))
+        for i in range(SPLIT_TILES, N_TILES):
+            y = psum.tile([P, T], F32, name="bank")
+            y_matmul(y, i, slice(0, T))
+            add_prev(y, i, slice(0, T), slice(0, T))

from contextlib import ExitStack

import concourse.mybir as mybir

K, L, R, M, T = 1536, 1536, 512, 1536, 512
FLOPS = 2 * (K * R * T + L * R * T + R * M * T)

F32 = mybir.dt.float32
BF16 = mybir.dt.bfloat16
I32 = mybir.dt.int32
U32 = mybir.dt.uint32
U8 = mybir.dt.uint8
E4M3 = mybir.dt.float8_e4m3fn_x4
E5M2 = mybir.dt.float8_e5m2_x4
E2M1 = mybir.dt.float4_e2m1fn_x4

P = 128
PACK = 4
K_PASS = P * PACK
PASSES = K // K_PASS
CHUNK = 128
CHUNKS = T // CHUNK
N_TILES = M // P
PREV_GROUP = 4
HALF = T // 2
STORE_TILES = (1, 1, 2, 2, 2, 2, 1, 1)
SPLIT_TILES = 2


def tile_mix_bilin_fm_res_kernel(tc, x, wx, c, wc, w_words, w_scales, prev, out):
    nc = tc.nc
    with ExitStack() as ctx:
        sb = ctx.enter_context(tc.tile_pool(name="sb", bufs=1))
        psum = ctx.enter_context(tc.psum_pool(name="psum", bufs=8))
        ctx.enter_context(tc.manual_schedule())

        def load_pass(src, g, name, cols=slice(0, T)):
            raw = sb.tile([P, PACK, cols.stop - cols.start], F32, name=name)
            nc.sync.dma_start(
                out=raw[:], in_=src[g * K_PASS : (g + 1) * K_PASS, cols].rearrange("(p j) w -> p j w", j=PACK)
            )
            return raw

        def mx_tiles(name):
            codes = sb.tile([P, T], U32, name=name + "_codes", align_bytes=64)
            scales = sb.tile([P, T], U8, name=name + "_scales", align_bytes=64)
            return codes, scales

        def interleave(copy, dst, src):
            copy(
                out=dst.rearrange("p (c i j) -> p c j i", i=4, j=PACK),
                in_=src.rearrange("p j (c i) -> p c j i", i=4),
            )

        def group_acts(raw):
            grouped = sb.tile([P, PACK * T], BF16, name="grouped_acts", bufs=2, align_bytes=64)
            interleave(nc.scalar.copy, grouped[:], raw[:])
            return grouped

        def group_weights(raw):
            halves = []
            for u in range(2):
                half = sb.tile([P, 2 * PACK * P], BF16, name="weight_half%d" % u, bufs=2, align_bytes=64)
                nc.vector.tensor_copy(
                    out=half[:].rearrange("p (s m j) -> p m j s", s=2, j=PACK),
                    in_=raw[:].rearrange("p j (m s) -> p m j s", s=PACK)[:, :, :, 2 * u : 2 * u + 2],
                )
                halves.append(half)
            return halves

        def quantize_weights(operand, halves):
            for u in range(2):
                quantize(operand, E4M3, halves[u], span(u, R // 2))

        def quantize(operand, fmt, grouped, cols=slice(0, T)):
            codes, scales = operand
            nc.vector.quantize_mx(out=codes[:, cols].bitcast(fmt), scales=scales[:, cols], in_=grouped[:])

        def matmul(acc, lhs, lhs_cols, rhs, rhs_fmt, rhs_cols, start, stop):
            nc.tensor.matmul_mx(
                out=acc,
                lhsT=lhs[0][:, lhs_cols].bitcast(E4M3),
                lhsT_scale=lhs[1][:, lhs_cols],
                rhs=rhs[0][:, rhs_cols].bitcast(rhs_fmt),
                rhs_scale=rhs[1][:, rhs_cols],
                start=start,
                stop=stop,
            )

        def span(i, width):
            return slice(i * width, (i + 1) * width)

        plane_raw = sb.tile([P, M], U8)
        nc.vector.memset(plane_raw[:].bitcast(I32), 0)
        words_raw = sb.tile([P, 2 * M], U8)
        nc.sync.dma_start(out=words_raw[:].bitcast(I32), in_=w_words[0].bitcast(I32))
        c_raw, wc_raw = [], []
        for g in range(PASSES):
            c_raw.append(load_pass(c, g, "c_raw%d" % g))
            if g == 0:
                for q in range(4):
                    nc.sync.dma_start(
                        out=plane_raw[32 * q : 32 * q + 4, :].bitcast(I32),
                        in_=w_scales[0, 4 * q : 4 * q + 4, :].bitcast(I32),
                    )
            wc_raw.append(load_pass(wc, g, "wc_raw%d" % g))
        wx_raw = [load_pass(wx, g, "wx_raw%d" % g) for g in range(PASSES)]
        x_raw = [load_pass(x, g, "x_raw%d" % g) for g in range(PASSES)]
        prev_sb = []
        for g in range(N_TILES // PREV_GROUP):
            rows = sb.tile([P, PREV_GROUP, T], F32, name="prev%d" % g)
            nc.sync.dma_start(
                out=rows[:], in_=prev[span(g, PREV_GROUP * P), :].rearrange("(p i) t -> p i t", p=P)
            )
            prev_sb.append(rows)

        w_codes = sb.tile([P, 2 * M], U8, align_bytes=64)
        w_plane = sb.tile([P, M], U8, align_bytes=64)
        nc.vector.tensor_copy(
            out=w_codes[:].rearrange("p (g i m b) -> p g m i b", i=PREV_GROUP, m=P, b=2),
            in_=words_raw[:].rearrange("p (g m i b) -> p g m i b", i=PREV_GROUP, m=P, b=2),
        )
        nc.vector.tensor_copy(
            out=w_plane[:].rearrange("p (g i m) -> p g m i", i=PREV_GROUP, m=P),
            in_=plane_raw[:].rearrange("p (g m i) -> p g m i", i=PREV_GROUP, m=P),
        )

        pc_banks = [psum.tile([P, T], F32, name="bank") for s in range(PACK)]
        for g in range(PASSES):
            c_q, wc_q = mx_tiles("c%d" % g), mx_tiles("wc%d" % g)
            c_grouped = group_acts(c_raw[g])
            wc_grouped = group_weights(wc_raw[g])
            quantize(c_q, E5M2, c_grouped)
            quantize_weights(wc_q, wc_grouped)
            for s in range(PACK):
                matmul(pc_banks[s][:], wc_q, span(s, P), c_q, E5M2, slice(0, T), g == 0, g == PASSES - 1)
        pc_rows = sb.tile([P, PACK, T], F32)
        for s in range(PACK):
            nc.scalar.copy(out=pc_rows[:, s, :], in_=pc_banks[s][:])
        pc_grouped = sb.tile([P, PACK * T], F32)
        interleave(nc.scalar.copy, pc_grouped[:], pc_rows[:])

        px_banks = [psum.tile([P, PACK, CHUNK], F32, name="bank") for b in range(CHUNKS)]

        def px_pass(g, b, wx_q, x_q):
            for s in range(PACK):
                first = g == 0 and s == 0
                last = g == PASSES - 1 and s == PACK - 1
                matmul(px_banks[b][:, s, :], wx_q, span(s, P), x_q, E4M3, span(b, CHUNK), first, last)

        wx_qs = []
        for g in range(PASSES):
            wx_q = mx_tiles("wx%d" % g)
            quantize_weights(wx_q, group_weights(wx_raw[g]))
            wx_qs.append(wx_q)

        for g in range(PASSES - 1):
            x_q = mx_tiles("x%d" % g)
            halves = []
            for u, copy in enumerate((nc.scalar.copy, nc.vector.tensor_copy)):
                half = sb.tile([P, PACK * HALF], BF16, name="x_half%d" % u, bufs=2, align_bytes=64)
                interleave(copy, half[:], x_raw[g][:, :, span(u, HALF)])
                halves.append(half)
            for u in (1, 0):
                quantize(x_q, E4M3, halves[u], span(u, HALF))
                for b in (2 * u, 2 * u + 1):
                    px_pass(g, b, wx_qs[g], x_q)

        g = PASSES - 1
        wx_q, x_q, h_q = wx_qs[g], mx_tiles("x%d" % g), mx_tiles("h")
        x_chunks, h_chunks = {}, []

        def group_chunk(copy, b):
            chunk = sb.tile([P, PACK * CHUNK], BF16, name="x_chunk%d" % b, align_bytes=64)
            interleave(copy, chunk[:], x_raw[g][:, :, span(b, CHUNK)])
            x_chunks[b] = chunk

        def finish_px(b):
            quantize(x_q, E4M3, x_chunks[b], span(b, CHUNK))
            px_pass(g, b, wx_q, x_q)

        def multiply(b):
            chunk = sb.tile([P, PACK * CHUNK], BF16, name="h_chunk%d" % b, align_bytes=64)
            nc.vector.tensor_tensor(
                out=chunk[:].rearrange("p (t s) -> p t s", s=PACK),
                in0=px_banks[b][:].rearrange("p s t -> p t s"),
                in1=pc_grouped[:, span(b, PACK * CHUNK)].rearrange("p (t s) -> p t s", s=PACK),
                op=mybir.AluOpType.mult,
            )
            h_chunks.append(chunk)

        def quantize_h(b):
            quantize(h_q, E4M3, h_chunks[b], span(b, CHUNK))

        def y_matmul(bank, i, cols):
            nc.tensor.matmul_mx(
                out=bank[:, cols],
                lhsT=w_codes[:, span(i, 2 * P)].bitcast(E2M1),
                lhsT_scale=w_plane[:, span(i, P)],
                rhs=h_q[0][:, cols].bitcast(E4M3),
                rhs_scale=h_q[1][:, cols],
                start=True,
                stop=True,
            )

        results, stores = [], {}
        for count in STORE_TILES:
            first = len(results)
            result = sb.tile([P, count, T], F32, name="result%d" % first)
            results.extend(result[:, j, :] for j in range(count))
            group, slot = divmod(first, PREV_GROUP)
            rows = out[span(group, PREV_GROUP * P), :].rearrange("(p i) t -> p i t", p=P)
            stores[first + count - 1] = (rows[:, slot : slot + count, :], result)

        def add_prev(bank, i, cols, bank_cols):
            nc.vector.tensor_tensor(
                out=results[i][:, cols],
                in0=bank[:, bank_cols],
                in1=prev_sb[i // PREV_GROUP][:, i % PREV_GROUP, cols],
                op=mybir.AluOpType.add,
            )
            if cols.stop == T and i in stores:
                rows, result = stores[i]
                nc.sync.dma_start(out=rows, in_=result[:])

        def y_half_matmul(bank, i, u):
            nc.tensor.matmul_mx(
                out=bank[:, span(i, HALF)],
                lhsT=w_codes[:, span(i, 2 * P)].bitcast(E2M1),
                lhsT_scale=w_plane[:, span(i, P)],
                rhs=h_q[0][:, span(u, HALF)].bitcast(E4M3),
                rhs_scale=h_q[1][:, span(u, HALF)],
                start=True,
                stop=True,
            )

        group_chunk(nc.vector.tensor_copy, 0)
        group_chunk(nc.vector.tensor_copy, 1)
        group_chunk(nc.scalar.copy, 2)
        group_chunk(nc.scalar.copy, 3)
        for b in range(CHUNKS):
            finish_px(b)
        multiply(0)
        multiply(1)
        quantize_h(0)
        multiply(2)
        quantize_h(1)
        early = psum.tile([P, T], F32, name="bank")
        for i in range(SPLIT_TILES):
            y_half_matmul(early, i, 0)
        multiply(3)
        quantize_h(2)
        quantize_h(3)
        for i in range(SPLIT_TILES):
            add_prev(early, i, span(0, HALF), span(i, HALF))
        for i in range(SPLIT_TILES):
            late = psum.tile([P, HALF], F32, name="bank")
            nc.tensor.matmul_mx(
                out=late[:],
                lhsT=w_codes[:, span(i, 2 * P)].bitcast(E2M1),
                lhsT_scale=w_plane[:, span(i, P)],
                rhs=h_q[0][:, span(1, HALF)].bitcast(E4M3),
                rhs_scale=h_q[1][:, span(1, HALF)],
                start=True,
                stop=True,
            )
            add_prev(late, i, span(1, HALF), span(0, HALF))
        for i in range(SPLIT_TILES, N_TILES):
            y = psum.tile([P, T], F32, name="bank")
            y_matmul(y, i, slice(0, T))
            add_prev(y, i, slice(0, T), slice(0, T))
